import numpy as np
import ml_dtypes


def mxq(x, axis, fmt="e4m3"):
    dtype, down = {"e4m3": (ml_dtypes.float8_e4m3fn, 7), "e5m2": (ml_dtypes.float8_e5m2, 14)}[fmt]
    v = np.moveaxis(np.asarray(x, np.float32).astype(ml_dtypes.bfloat16).astype(np.float64), axis, -1)
    blocks = v.reshape(v.shape[:-1] + (-1, 32))
    amax = np.abs(blocks).max(-1, keepdims=True)
    byte = np.maximum(np.where(amax > 0, np.frexp(amax)[1] - 1 + 127, 0) - down, 1)
    scale = np.exp2(byte - 127.0)
    codes = (blocks / scale).astype(np.float32).astype(dtype).astype(np.float64)
    return np.moveaxis((codes * scale).reshape(v.shape), -1, axis)


WIDE = False


def mx_kscale(k):
    if not WIDE:
        return np.ones(k)
    levels = np.array([10, -10, 5, -5, 0])
    if k % 512:
        return np.exp2(np.random.permutation(np.resize(levels, k // 32))).repeat(32)
    a = np.empty((k // 512, 16))
    for p in range(k // 512):
        a[p, :8] = np.random.permutation(np.resize(levels, 8))
        for g in range(8):
            far = levels[np.abs(levels - a[p, g]) >= 10]
            a[p, g + 8] = far[np.random.randint(len(far))]
    return np.exp2(a.ravel()).repeat(32)


def f64(x):
    return np.asarray(x).astype(np.float64)


def striped(idx):
    return np.tile(np.asarray(idx).reshape(-1, 16).T, (8, 1)).astype(np.uint16)


def unstriped(offs):
    return offs[:16].T.reshape(-1).astype(np.int64)


E2M1 = np.array([0.0, 0.5, 1.0, 1.5, 2.0, 3.0, 4.0, 6.0, -0.0, -0.5, -1.0, -1.5, -2.0, -3.0, -4.0, -6.0])


def pack_weight(w, fmt):
    k, n = w.shape
    w = f64(np.asarray(w, np.float32).astype(ml_dtypes.bfloat16)).reshape(k // 32, 32, n)
    amax = np.abs(w).max(1)
    if fmt == "e4m3":
        byte = np.frexp(amax)[1] - 1 + 127 - 7
    else:
        mant, ex = np.frexp(amax / 6.0)
        byte = np.where(mant > 0.5, ex, ex - 1) + 127
    byte = np.clip(np.where(amax > 0, byte, 1), 1, 254)
    scaled = (w * np.exp2(127.0 - byte)[:, None, :]).reshape(k, n).astype(np.float32)
    by_word = np.ascontiguousarray(scaled.reshape(k // 512, 128, 4, n).transpose(0, 1, 3, 2))
    if fmt == "e4m3":
        words = by_word.astype(ml_dtypes.float8_e4m3fn).view(np.uint8)
    else:
        c = by_word.astype(ml_dtypes.float4_e2m1fn).view(np.uint8) & 0xF
        words = (c[..., 0::2] | (c[..., 1::2] << 4)).reshape(k // 512, 128, 2 * n)
    return np.ascontiguousarray(words), np.ascontiguousarray(byte.astype(np.uint8).reshape(k // 512, 16, n))


def unpack_weight(words, scales, fmt):
    g, _, n = scales.shape
    words = np.ascontiguousarray(words).reshape(g, 128, n, -1)
    if fmt == "e4m3":
        vals = words.view(ml_dtypes.float8_e4m3fn).astype(np.float64)
    else:
        nib = np.empty((g, 128, n, 4), np.uint8)
        nib[..., 0::2] = words & 0xF
        nib[..., 1::2] = words >> 4
        vals = E2M1[nib]
    vals = vals * np.repeat(np.exp2(scales.astype(np.float64) - 127.0), 8, axis=1)[..., None]
    return vals.transpose(0, 1, 3, 2).reshape(g * 512, n)


D, E, T, I, Q, G, U = 512, 512, 2048, 512, 128, 64, 256


def setup_inputs():
    n = np.random.standard_normal
    idx = np.random.permutation(T)[:I]
    idx2 = np.random.permutation(U)[:G]
    fd = mx_kscale(D)
    fe = mx_kscale(E)
    keysp = pack_weight(n((D, T)) / fd[:, None], "e4m3")
    valsp = pack_weight(n((E, T)) / fe[:, None], "e4m3")
    return {
        "query": (n((D, Q)) * 0.6 / np.sqrt(D) * fd[:, None]).astype(np.float32),
        "keys_words": keysp[0],
        "keys_scales": keysp[1],
        "gout": (n((E, Q)) * 1 / np.sqrt(E) * fe[:, None]).astype(np.float32),
        "vals_words": valsp[0],
        "vals_scales": valsp[1],
        "pofs": (n((E, U)) / fe[:, None]).astype(np.float32),
        "pf": (np.random.uniform(0.5, 2.0, (Q, 1))).astype(np.float32),
        "old": (0.5 * n((Q, T))).astype(np.float32),
        "offs": striped(idx),
        "offs2": striped(idx2),
    }


def reference(query, keys_words, keys_scales, gout, vals_words, vals_scales, pofs, pf, old, offs, offs2):
    idx = unstriped(offs)
    idx2 = unstriped(offs2)
    keysu = unpack_weight(keys_words, keys_scales, "e4m3")
    valsu = unpack_weight(vals_words, vals_scales, "e4m3")
    queryq = mxq(f64(query), 0, "e4m3")
    keysidxg = keysu[:, idx]
    a = queryq.T @ keysidxg
    p = np.exp(a - np.max(a, axis=1, keepdims=True))
    z = np.sum(p, axis=1, keepdims=True)
    s = p.reshape(Q, G, I // G).sum(axis=2) * f64(pf)
    goutq = mxq(f64(gout), 0, "e4m3")
    valsidxg = valsu[:, idx]
    c0 = goutq.T @ valsidxg
    pofsidx2q = mxq(f64(pofs)[:, idx2], 0, "e4m3")
    c1 = goutq.T @ pofsidx2q
    ds = 1.0 / z * c1
    e1 = ds * f64(pf)
    r1 = np.repeat(e1, I // G, axis=1)
    dz = (np.sum(p * c0, axis=1, keepdims=True) + np.sum(s * c1, axis=1, keepdims=True)) / np.square(z) * (-1.0)
    dp = 1.0 / z * c0 + r1 + dz
    da = dp * p
    gs = da * 512.0
    gf = np.zeros((Q, T))
    gf[:, idx] = gs
    y = f64(old) + gf
    return y

from contextlib import ExitStack

import concourse.mybir as mybir

D, E, T, I, Q, G, U = 512, 512, 2048, 512, 128, 64, 256
FLOPS = 2 * Q * (D * I + E * I + E * G)

F32 = mybir.dt.float32
BF16 = mybir.dt.bfloat16
I32 = mybir.dt.int32
U32 = mybir.dt.uint32
U16 = mybir.dt.uint16
U8 = mybir.dt.uint8
FP8X4 = mybir.dt.float8_e4m3fn_x4
ALU = mybir.AluOpType
ACT = mybir.ActivationFunctionType
AX = mybir.AxisListType

P = 128
PACK = 4
PAGE = I // G
HALF = I // 2
VALS_ROW = 4
STORE_WIDTHS = (256, 512, 512, 512, 256)


def tile_attend_bpageoffsets_s_kernel(tc, query, keys_words, keys_scales, gout, vals_words, vals_scales, pofs, pf, old, offs, offs2, out):
    nc = tc.nc
    with ExitStack() as ctx:
        sb = ctx.enter_context(tc.tile_pool(name="sb", bufs=1))
        ps = ctx.enter_context(tc.psum_pool(name="ps", bufs=1))

        slots = sb.tile([P, I // 16], U16, name="slots")
        pages = sb.tile([P, G // 16], U16, name="pages")
        key_bytes = sb.tile([P, T], U8, name="key_bytes", tag="key_bytes_then_pf", align_bytes=64)
        val_bytes = sb.tile([P, T], U8, name="val_bytes", tag="val_bytes_then_max", align_bytes=64)
        placed = sb.tile([P, T], F32, name="placed", align_bytes=64)
        q_raw = sb.tile([P, PACK, Q], F32, name="q_raw", align_bytes=64)
        g_raw = sb.tile([P, PACK, Q], F32, name="g_raw", align_bytes=64)
        pofs_raw = sb.tile([P, PACK, U], F32, name="pofs_raw", align_bytes=64)
        key_words = sb.tile([P, T], I32, name="key_words", tag="keys_then_old", align_bytes=64)
        val_words = sb.tile([P, T], I32, name="val_words", align_bytes=64)

        nc.vector.memset(key_bytes[:].bitcast(I32), 0)
        nc.vector.memset(val_bytes[:].bitcast(I32), 0)
        nc.vector.memset(placed[:], 0.0)

        pofs_half = sb.tile([P, 3 * U], BF16, name="pofs_half", tag="pofs_half_then_p", align_bytes=64)
        nc.vector.memset(pofs_half[:, 2 * U : 3 * U], 0.0)

        def load_scale_rows(queue, plane, rows, first):
            for r in range(4):
                queue.dma_start(out=plane[first + r : P : 32, :].bitcast(I32), in_=rows[0, r:16:4, :].bitcast(I32))

        nc.sync.dma_start(slots[:], offs)
        nc.sync.dma_start(out=q_raw[:], in_=query.rearrange("(p j) w -> p j w", j=PACK))
        nc.sync.dma_start(pages[:], offs2)
        load_scale_rows(nc.sync, key_bytes, keys_scales, 0)
        nc.sync.dma_start(out=key_words[:], in_=keys_words[0].rearrange("p n t -> p (n t)").bitcast(I32))
        load_scale_rows(nc.sync, val_bytes, vals_scales, VALS_ROW)
        nc.sync.dma_start(out=g_raw[:], in_=gout.rearrange("(p j) w -> p j w", j=PACK))
        nc.sync.dma_start(out=pofs_raw[:], in_=pofs.rearrange("(p j) w -> p j w", j=PACK))
        nc.sync.dma_start(out=val_words[:], in_=vals_words[0].rearrange("p n t -> p (n t)").bitcast(I32))

        def weave(raw, name):
            woven = sb.tile([P, Q, PACK], BF16, name=name, align_bytes=64)
            nc.scalar.copy(
                out=woven[:].rearrange("p (c i) t -> p c t i", i=4),
                in_=raw[:].rearrange("p t (c i) -> p c t i", i=4),
            )
            return woven

        def quantize(woven, width, name):
            codes = sb.tile([P, width], U32, name=name + "_codes", align_bytes=64)
            scales = sb.tile([P, width], U8, name=name + "_scales", align_bytes=64)
            nc.vector.quantize_mx(out=codes[:].bitcast(FP8X4), scales=scales[:], in_=woven[:].rearrange("p w j -> p (w j)"))
            return codes, scales

        k_scales = sb.tile([P, I], U8, name="k_scales", align_bytes=64)
        v_scales = sb.tile([P, I], U8, name="v_scales", align_bytes=64)
        k_codes = sb.tile([P, I], U32, name="k_codes", align_bytes=64)

        q_woven = weave(q_raw, "q_woven")
        nc.vector.tensor_copy(k_scales[:], key_bytes[:].indirect(slots[:]))
        pf_col = sb.tile([P, 1], F32, name="pf_col", tag="key_bytes_then_pf", align_bytes=64)
        nc.scalar.dma_start(out=pf_col[:], in_=pf)
        q_codes, q_scales = quantize(q_woven, Q, "q")
        nc.vector.tensor_copy(k_codes[:], key_words[:].bitcast(U32).indirect(slots[:]))
        nc.vector.tensor_copy(v_scales[:], val_bytes[:].indirect(slots[:]))

        old_sb = sb.tile([P, T], F32, name="old_sb", tag="keys_then_old", align_bytes=64)
        nc.sync.dma_start(out=old_sb[:], in_=old)

        a_ps = ps.tile([P, I], F32, name="a_ps")
        nc.tensor.matmul_mx(out=a_ps[:], lhsT=q_codes[:].bitcast(FP8X4), lhsT_scale=q_scales[:],
                            rhs=k_codes[:].bitcast(FP8X4), rhs_scale=k_scales[:], start=True, stop=True)

        g_woven = weave(g_raw, "g_woven")
        g_codes, g_scales = quantize(g_woven, Q, "g")

        neg_max = sb.tile([P, 1], F32, name="neg_max", tag="val_bytes_then_max", align_bytes=64)
        nc.vector.tensor_reduce(out=neg_max[:], in_=a_ps[:], axis=AX.X, op=ALU.max, negate=True)

        pofs_woven = sb.tile([P, G, PACK], BF16, name="pofs_woven", tag="half_codes0", align_bytes=64)
        for j in (0, 1):
            nc.vector.tensor_copy(pofs_woven[:, :, j], pofs_raw[:, j, :].indirect(pages[:]))
        nc.scalar.copy(out=pofs_half[:, 0 : 2 * U], in_=pofs_raw[:, 2:4, :].rearrange("p j u -> p (j u)"))
        for j in (2, 3):
            first = (j - 2) * U
            nc.scalar.activation(pofs_woven[:, :, j], pofs_half[:, first : first + 2 * U].indirect(pages[:]), ACT.Copy)
        p = sb.tile([P, I], F32, name="p", tag="pofs_half_then_p", align_bytes=64)
        z = sb.tile([P, 1], F32, name="z")
        nc.scalar.activation(out=p[:], in_=a_ps[:], func=ACT.Exp, bias=neg_max[:], scale=1.0, accum_out=z[:])
        o_codes, o_scales = quantize(pofs_woven, G, "o")
        c1_ps = ps.tile([P, G], F32, name="c1_ps")
        nc.tensor.matmul_mx(out=c1_ps[:], lhsT=g_codes[:].bitcast(FP8X4), lhsT_scale=g_scales[:],
                            rhs=o_codes[:].bitcast(FP8X4), rhs_scale=o_scales[:], start=True, stop=True)
        page_term = sb.tile([P, G], F32, name="page_term")
        nc.scalar.activation(out=page_term[:], in_=c1_ps[:], func=ACT.Copy, scale=pf_col[:])

        c0_ps = []
        for h in range(2):
            cols = slice(h * HALF, (h + 1) * HALF)
            v_codes = sb.tile([P, HALF], U32, name="v_codes%d" % h, tag="half_codes%d" % h, align_bytes=64)
            nc.vector.tensor_copy(v_codes[:], val_words[:].bitcast(U32).indirect(slots[:, h * HALF // 16 : (h + 1) * HALF // 16]))
            bank = ps.tile([P, HALF], F32, name="c0_ps%d" % h)
            nc.tensor.matmul_mx(out=bank[:], lhsT=g_codes[:].bitcast(FP8X4), lhsT_scale=g_scales[:],
                                rhs=v_codes[:].bitcast(FP8X4), rhs_scale=v_scales[VALS_ROW:P, cols], start=True, stop=True)
            c0_ps.append(bank)

        inv_z = sb.tile([P, 1], F32, name="inv_z")
        nc.vector.reciprocal(out=inv_z[:], in_=z[:])
        gain = sb.tile([P, 1], F32, name="gain")
        nc.scalar.activation(out=gain[:], in_=inv_z[:], func=ACT.Copy, scale=512.0)

        c = sb.tile([P, I], F32, name="c", align_bytes=64)
        for h in range(2):
            nc.vector.tensor_tensor(
                out=c[:, h * HALF : (h + 1) * HALF].rearrange("p (g s) -> p g s", s=PAGE),
                in0=c0_ps[h][:].rearrange("p (g s) -> p g s", s=PAGE),
                in1=page_term[:, h * G // 2 : (h + 1) * G // 2].unsqueeze(2).to_broadcast([P, G // 2, PAGE]),
                op=ALU.add,
            )
        weighted = sb.tile([P, I], F32, name="weighted", align_bytes=64)
        mean = sb.tile([P, 1], F32, name="mean")
        nc.vector.scalar_tensor_tensor(out=weighted[:], in0=p[:], scalar=inv_z[:], in1=c[:], op0=ALU.mult, op1=ALU.mult, accum_out=mean[:])
        centred = sb.tile([P, I], F32, name="centred", align_bytes=64)
        nc.vector.tensor_scalar(out=centred[:], in0=c[:], scalar1=mean[:], scalar2=gain[:], op0=ALU.subtract, op1=ALU.mult)
        nc.vector.tensor_tensor(placed[:].indirect(slots[:]), centred[:], p[:], ALU.mult)

        start = 0
        for n, width in enumerate(STORE_WIDTHS):
            cols = slice(start, start + width)
            total = sb.tile([P, width], F32, name="total%d" % n, align_bytes=64)
            nc.vector.tensor_tensor(out=total[:], in0=placed[:, cols], in1=old_sb[:, cols], op=ALU.add)
            nc.sync.dma_start(out=out[:, cols], in_=total[:])
            start = start + width
